import numpy as np
import ml_dtypes


def mxq(x, axis, fmt="e4m3"):
    dtype, down = {"e4m3": (ml_dtypes.float8_e4m3fn, 7), "e5m2": (ml_dtypes.float8_e5m2, 14)}[fmt]
    v = np.moveaxis(np.asarray(x, np.float32).astype(ml_dtypes.bfloat16).astype(np.float64), axis, -1)
    blocks = v.reshape(v.shape[:-1] + (-1, 32))
    amax = np.abs(blocks).max(-1, keepdims=True)
    byte = np.maximum(np.where(amax > 0, np.frexp(amax)[1] - 1 + 127, 0) - down, 1)
    scale = np.exp2(byte - 127.0)
    codes = (blocks / scale).astype(np.float32).astype(dtype).astype(np.float64)
    return np.moveaxis((codes * scale).reshape(v.shape), -1, axis)


WIDE = False


def mx_kscale(k):
    if not WIDE:
        return np.ones(k)
    levels = np.array([10, -10, 5, -5, 0])
    if k % 512:
        return np.exp2(np.random.permutation(np.resize(levels, k // 32))).repeat(32)
    a = np.empty((k // 512, 16))
    for p in range(k // 512):
        a[p, :8] = np.random.permutation(np.resize(levels, 8))
        for g in range(8):
            far = levels[np.abs(levels - a[p, g]) >= 10]
            a[p, g + 8] = far[np.random.randint(len(far))]
    return np.exp2(a.ravel()).repeat(32)


def f64(x):
    return np.asarray(x).astype(np.float64)


def striped8(idx):
    return np.concatenate([x.reshape(-1, 16).T for x in idx]).astype(np.uint16)


def runs(offs, k):
    lists = np.stack([offs[16 * r : 16 * r + 16].T.reshape(-1) for r in range(8)]).astype(np.int64)
    return lists[np.arange(k) % 512 // 64]


def pack_weight(w):
    k, n = w.shape
    w = f64(np.asarray(w, np.float32).astype(ml_dtypes.bfloat16)).reshape(k // 32, 32, n)
    amax = np.abs(w).max(1)
    byte = np.clip(np.where(amax > 0, np.frexp(amax)[1] - 1 + 127 - 7, 1), 1, 254)
    scaled = (w * np.exp2(127.0 - byte)[:, None, :]).reshape(k, n).astype(np.float32)
    words = np.ascontiguousarray(scaled.reshape(k // 512, 128, 4, n).transpose(0, 1, 3, 2)).astype(ml_dtypes.float8_e4m3fn).view(np.uint8)
    return words, np.ascontiguousarray(byte.astype(np.uint8).reshape(k // 512, 16, n))


def unpack_weight(words, scales):
    g, p, n, _ = words.shape
    vals = np.ascontiguousarray(words).view(ml_dtypes.float8_e4m3fn).astype(np.float64) * np.repeat(np.exp2(scales.astype(np.float64) - 127.0), 8, axis=1)[..., None]
    return vals.transpose(0, 1, 3, 2).reshape(g * 512, n)


def gelu(v):
    return 0.5 * v * (1.0 + np.tanh(np.sqrt(2.0 / np.pi) * (v + 0.044715 * v**3)))


K, T, S, H, N = 1024, 2048, 512, 512, 256


def setup_inputs():
    n = np.random.standard_normal
    s = mx_kscale(K)[:, None]
    u = mx_kscale(H)
    packed_xT = pack_weight(n((K, T)) * s)
    packed_w1 = pack_weight(n((K, N)) / np.sqrt(2 * K) / s)
    packed_w3 = pack_weight(n((H, N)) / np.sqrt(2 * H) / u[:, None])
    return {
        "x_words": packed_xT[0],
        "x_scales": packed_xT[1],
        "w1_words": packed_w1[0],
        "w1_scales": packed_w1[1],
        "w2": (n((K, H)) / np.sqrt(K) / s * u).astype(np.float32),
        "w3_words": packed_w3[0],
        "w3_scales": packed_w3[1],
        "offs": striped8(np.stack([np.random.permutation(T)[:S] for _ in range(8)])),
    }


def reference(x_words, x_scales, w1_words, w1_scales, w2, w3_words, w3_scales, offs):
    xq = unpack_weight(x_words, x_scales)[np.arange(K)[:, None], runs(offs, K)]
    h = gelu(mxq(f64(w2), 0, "e4m3").T @ xq)
    return unpack_weight(w1_words, w1_scales).T @ xq + unpack_weight(w3_words, w3_scales).T @ mxq(h, 0, "e4m3")

@@ -1,0 +1,183 @@
+from contextlib import ExitStack
+
+import concourse.mybir as mybir
+
+K, T, S, H, N = 1024, 2048, 512, 512, 256
+FLOPS = 2 * S * (K * H + K * N + H * N)
+
+F32 = mybir.dt.float32
+BF16 = mybir.dt.bfloat16
+I32 = mybir.dt.int32
+U32 = mybir.dt.uint32
+U16 = mybir.dt.uint16
+U8 = mybir.dt.uint8
+FP8X4 = mybir.dt.float8_e4m3fn_x4
+GELU = mybir.ActivationFunctionType.Gelu_apprx_tanh
+
+P = 128
+PACK = 4
+PASSES = K // (P * PACK)
+CHUNK = 128
+CHUNKS = S // CHUNK
+HALF = 256
+M_TILES = N // P
+
+
+def tile_picked_phlora_gelu_p_kernel(
+    tc, x_words, x_scales, w1_words, w1_scales, w2, w3_words, w3_scales, offs, out
+):
+    nc = tc.nc
+    with ExitStack() as ctx:
+        sb = ctx.enter_context(tc.tile_pool(name="sb", bufs=1))
+        ps = ctx.enter_context(tc.psum_pool(name="ps", bufs=1))
+
+        def tile(name, shape, dtype, tag=None):
+            return sb.tile(shape, dtype, name=name, tag=tag or name, align_bytes=64)
+
+        offsets = tile("offsets", [P, S // 16], U16)
+        nc.sync.dma_start(offsets[:], offs)
+
+        byte_win = [tile("byte_win%d" % z, [P, T], U8) for z in range(PASSES)]
+        nc.vector.memset(byte_win[0][:].bitcast(I32), 0)
+        nc.gpsimd.memset(byte_win[1][:].bitcast(I32), 0)
+        for z in range(PASSES):
+            nc.scalar.dma_start(byte_win[z][:].bitcast(I32)[0:P:8, :], x_scales[z].bitcast(I32))
+
+        word_win = [tile("word_win%d" % z, [P, T], U32) for z in range(PASSES)]
+        w2_raw = [tile("w2_raw%d" % z, [P, PACK, H], F32) for z in range(PASSES)]
+
+        def load_words(z):
+            nc.sync.dma_start(word_win[z][:].bitcast(I32), x_words[z].rearrange("p n t -> p (n t)").bitcast(I32))
+
+        def load_w2(z):
+            nc.sync.dma_start(w2_raw[z][:], w2[z * 512 : (z + 1) * 512, :].rearrange("(p j) c -> p j c", j=PACK))
+
+        load_words(0)
+        load_w2(0)
+        load_w2(1)
+        load_words(1)
+
+        w1_plane = tile("w1_plane", [P, N], U8)
+        w3_plane = tile("w3_plane", [P, N], U8)
+        nc.gpsimd.memset(w1_plane[:].bitcast(I32), 0)
+        nc.gpsimd.memset(w3_plane[:].bitcast(I32), 0)
+        for q in range(4):
+            nc.gpsimd.dma_start(
+                w1_plane[:].bitcast(I32)[32 * q : 32 * q + 8, :], w1_scales.bitcast(I32)[:, 4 * q : 4 * q + 4, :]
+            )
+        for q in range(4):
+            nc.gpsimd.dma_start(
+                w3_plane[:].bitcast(I32)[32 * q : 32 * q + 4, :], w3_scales.bitcast(I32)[0, 4 * q : 4 * q + 4, :]
+            )
+
+        picked_bytes = tile("picked_bytes", [P, PASSES * S], U8, tag="late")
+        for z in range(PASSES):
+            nc.vector.tensor_copy(picked_bytes[:, z * S : (z + 1) * S], byte_win[z][:].indirect(offsets[:]))
+        x_plane = tile("x_plane", [P, PASSES * S], U8)
+        nc.vector.tensor_copy(x_plane[:].bitcast(I32), picked_bytes[:].bitcast(I32))
+        for j in range(1, 4):
+            nc.scalar.dma_start(x_plane[:].bitcast(I32)[j:P:32, :], picked_bytes[:].bitcast(I32)[8 * j : P : 32, :])
+
+        w13 = tile("w13", [P, PASSES + 1, N], U32, tag="late")
+        nc.sync.dma_start(
+            w13[:].bitcast(I32)[:, 0:PASSES, :], w1_words.rearrange("z p n t -> p z (n t)").bitcast(I32)
+        )
+        nc.sync.dma_start(w13[:].bitcast(I32)[:, PASSES, :], w3_words[0].rearrange("p n t -> p (n t)").bitcast(I32))
+
+        picked = {}
+
+        def gather_words(z):
+            for u in range(S // HALF):
+                picked[z, u] = tile("picked%d_%d" % (z, u), [P, HALF], U32)
+                nc.vector.tensor_copy(picked[z, u][:], word_win[z][:].indirect(offsets[:, u * 16 : (u + 1) * 16]))
+
+        def tokens(z, c):
+            lo = (c % 2) * CHUNK
+            return (
+                picked[z, c // 2][:, lo : lo + CHUNK].bitcast(FP8X4),
+                x_plane[:, z * S + c * CHUNK : z * S + (c + 1) * CHUNK],
+            )
+
+        w2_codes, w2_plane = {}, {}
+
+        def quantize_w2(z):
+            grouped = []
+            src = w2_raw[z][:].rearrange("p j (m t) -> p m j t", t=PACK)
+            for u in range(2):
+                g = tile("w2_bf%d_%d" % (z, u), [P, 2 * P * PACK], BF16)
+                dst = g[:].rearrange("p (t m j) -> p m j t", t=2, j=PACK)
+                if u == 0:
+                    nc.vector.tensor_copy(dst, src[:, :, :, 0:2])
+                else:
+                    nc.scalar.copy(dst, src[:, :, :, 2:4])
+                grouped.append(g)
+            for u in range(2):
+                w2_codes[z, u] = tile("w2_codes%d_%d" % (z, u), [P, 2 * P], U32)
+                w2_plane[z, u] = tile("w2_plane%d_%d" % (z, u), [P, 2 * P], U8)
+                nc.vector.quantize_mx(out=w2_codes[z, u][:].bitcast(FP8X4), scales=w2_plane[z, u][:], in_=grouped[u][:])
+
+        h_acc = [ps.tile([P, PACK, CHUNK], F32, name="h_acc%d" % c, tag="h_acc%d" % c) for c in range(CHUNKS)]
+        o_acc = [ps.tile([P, M_TILES, CHUNK], F32, name="o_acc%d" % c, tag="o_acc%d" % c) for c in range(CHUNKS)]
+
+        def hidden_pass(z, c):
+            rhs, rhs_scale = tokens(z, c)
+            for t in range(PACK):
+                cols = slice((t % 2) * P, (t % 2 + 1) * P)
+                nc.tensor.matmul_mx(
+                    out=h_acc[c][:, t, :],
+                    lhsT=w2_codes[z, t // 2][:, cols].bitcast(FP8X4),
+                    lhsT_scale=w2_plane[z, t // 2][:, cols],
+                    rhs=rhs,
+                    rhs_scale=rhs_scale,
+                    start=(z == 0 and t == 0),
+                    stop=(z == PASSES - 1 and t == PACK - 1),
+                )
+
+        gather_words(0)
+        quantize_w2(0)
+        for c in range(CHUNKS):
+            hidden_pass(0, c)
+        quantize_w2(1)
+        gather_words(1)
+        for c in range(CHUNKS):
+            hidden_pass(1, c)
+
+        out_view = out.rearrange("(m p) n -> p m n", p=P)
+        h_codes, h_plane = [], []
+        for c in range(CHUNKS):
+            h_bf = tile("h_bf%d" % c, [P, CHUNK * PACK], BF16)
+            nc.scalar.activation(
+                h_bf[:].rearrange("p (n t) -> p n t", t=PACK), h_acc[c][:].rearrange("p t n -> p n t"), GELU
+            )
+            h_codes.append(tile("h_codes%d" % c, [P, CHUNK], U32))
+            h_plane.append(tile("h_plane%d" % c, [P, CHUNK], U8))
+            nc.vector.quantize_mx(out=h_codes[c][:].bitcast(FP8X4), scales=h_plane[c][:], in_=h_bf[:])
+
+        for c in range(CHUNKS):
+            for z in range(PASSES):
+                rhs, rhs_scale = tokens(z, c)
+                for m in range(M_TILES):
+                    cols = slice(m * P, (m + 1) * P)
+                    nc.tensor.matmul_mx(
+                        out=o_acc[c][:, m, :],
+                        lhsT=w13[:, z, cols].bitcast(FP8X4),
+                        lhsT_scale=w1_plane[4 * z : P, cols],
+                        rhs=rhs,
+                        rhs_scale=rhs_scale,
+                        start=(z == 0 and m == 0),
+                        stop=False,
+                    )
+            for m in range(M_TILES):
+                cols = slice(m * P, (m + 1) * P)
+                nc.tensor.matmul_mx(
+                    out=o_acc[c][:, m, :],
+                    lhsT=w13[:, PASSES, cols].bitcast(FP8X4),
+                    lhsT_scale=w3_plane[:, cols],
+                    rhs=h_codes[c][:].bitcast(FP8X4),
+                    rhs_scale=h_plane[c][:],
+                    start=False,
+                    stop=(m == M_TILES - 1),
+                )
+            result = tile("result%d" % c, [P, M_TILES, CHUNK], F32)
+            nc.vector.tensor_copy(result[:], o_acc[c][:])
+            nc.sync.dma_start(out_view[:, :, c * CHUNK : (c + 1) * CHUNK], result[:])

@@ -21,6 +21,7 @@ CHUNK = 128
 CHUNKS = S // CHUNK
 HALF = 256
 M_TILES = N // P
+SCALAR_M = 48
 
 
 def tile_picked_phlora_gelu_p_kernel(
@@ -35,54 +36,49 @@ def tile_picked_phlora_gelu_p_kernel(
             return sb.tile(shape, dtype, name=name, tag=tag or name, align_bytes=64)
 
         offsets = tile("offsets", [P, S // 16], U16)
+
+        byte_win = tile("byte_win", [P, T], U8)
+        nc.gpsimd.memset(byte_win[:].bitcast(I32), 0)
+
+        word_win = [tile("word_win0", [P, T], U32, tag="words")]
+        x_words32 = x_words.rearrange("z p n t -> z p (n t)").bitcast(I32)
+        nc.sync.dma_start(word_win[0][:].bitcast(I32)[:, 0:512], x_words32[0, :, 0:512])
         nc.sync.dma_start(offsets[:], offs)
+        nc.sync.dma_start(word_win[0][:].bitcast(I32)[:, 512:1024], x_words32[0, :, 512:1024])
+        x_rows = x_scales.bitcast(I32).rearrange("z (r e) c -> e r z c", e=2)
+        for e in range(2):
+            nc.sync.dma_start(byte_win[:].bitcast(I32)[e:P:8, :], x_rows[e])
+        nc.sync.dma_start(word_win[0][:].bitcast(I32)[:, 1024:T], x_words32[0, :, 1024:T])
 
-        byte_win = [tile("byte_win%d" % z, [P, T], U8) for z in range(PASSES)]
-        nc.vector.memset(byte_win[0][:].bitcast(I32), 0)
-        nc.gpsimd.memset(byte_win[1][:].bitcast(I32), 0)
-        for z in range(PASSES):
-            nc.scalar.dma_start(byte_win[z][:].bitcast(I32)[0:P:8, :], x_scales[z].bitcast(I32))
+        def load_w2(z, tag):
+            raw = tile("w2_raw%d" % z, [P, PACK, H], F32, tag=tag)
+            nc.sync.dma_start(raw[:], w2[z * 512 : (z + 1) * 512, :].rearrange("(p j) c -> p j c", j=PACK))
+            return raw
 
-        word_win = [tile("word_win%d" % z, [P, T], U32) for z in range(PASSES)]
-        w2_raw = [tile("w2_raw%d" % z, [P, PACK, H], F32) for z in range(PASSES)]
+        w2_raw = [load_w2(0, "first_w2"), load_w2(1, "second_w2")]
 
-        def load_words(z):
-            nc.sync.dma_start(word_win[z][:].bitcast(I32), x_words[z].rearrange("p n t -> p (n t)").bitcast(I32))
-
-        def load_w2(z):
-            nc.sync.dma_start(w2_raw[z][:], w2[z * 512 : (z + 1) * 512, :].rearrange("(p j) c -> p j c", j=PACK))
-
-        load_words(0)
-        load_w2(0)
-        load_w2(1)
-        load_words(1)
-
-        w1_plane = tile("w1_plane", [P, N], U8)
+        w1_plane = tile("w1_plane", [P, PASSES, N], U8)
         w3_plane = tile("w3_plane", [P, N], U8)
         nc.gpsimd.memset(w1_plane[:].bitcast(I32), 0)
         nc.gpsimd.memset(w3_plane[:].bitcast(I32), 0)
+        w1_rows = w1_scales.bitcast(I32).rearrange("z q c -> q z c")
         for q in range(4):
-            nc.gpsimd.dma_start(
-                w1_plane[:].bitcast(I32)[32 * q : 32 * q + 8, :], w1_scales.bitcast(I32)[:, 4 * q : 4 * q + 4, :]
-            )
+            nc.gpsimd.dma_start(w1_plane[:].bitcast(I32)[32 * q : 32 * q + 4, :, :], w1_rows[4 * q : 4 * q + 4])
         for q in range(4):
             nc.gpsimd.dma_start(
                 w3_plane[:].bitcast(I32)[32 * q : 32 * q + 4, :], w3_scales.bitcast(I32)[0, 4 * q : 4 * q + 4, :]
             )
 
-        picked_bytes = tile("picked_bytes", [P, PASSES * S], U8, tag="late")
+        picked_bytes = tile("picked_bytes", [P, S], U8, tag="last_words")
+        nc.vector.tensor_copy(picked_bytes[:], byte_win[:].indirect(offsets[:]))
+        x_plane = tile("x_plane", [P, S], U8)
+        x_plane32 = x_plane[:].bitcast(I32)
+        nc.vector.tensor_copy(x_plane32, picked_bytes[:].bitcast(I32))
         for z in range(PASSES):
-            nc.vector.tensor_copy(picked_bytes[:, z * S : (z + 1) * S], byte_win[z][:].indirect(offsets[:]))
-        x_plane = tile("x_plane", [P, PASSES * S], U8)
-        nc.vector.tensor_copy(x_plane[:].bitcast(I32), picked_bytes[:].bitcast(I32))
-        for j in range(1, 4):
-            nc.scalar.dma_start(x_plane[:].bitcast(I32)[j:P:32, :], picked_bytes[:].bitcast(I32)[8 * j : P : 32, :])
-
-        w13 = tile("w13", [P, PASSES + 1, N], U32, tag="late")
-        nc.sync.dma_start(
-            w13[:].bitcast(I32)[:, 0:PASSES, :], w1_words.rearrange("z p n t -> p z (n t)").bitcast(I32)
-        )
-        nc.sync.dma_start(w13[:].bitcast(I32)[:, PASSES, :], w3_words[0].rearrange("p n t -> p (n t)").bitcast(I32))
+            for e in range(2):
+                nc.sync.dma_start(x_plane32[8 * z + 2 + e : P : 32, :], x_plane32[8 * z + 16 + e : P : 32, :])
+        word_win.append(tile("word_win1", [P, T], U32, tag="last_words"))
+        nc.sync.dma_start(word_win[1][:].bitcast(I32), x_words32[1])
 
         picked = {}
 
@@ -95,26 +91,25 @@ def tile_picked_phlora_gelu_p_kernel(
             lo = (c % 2) * CHUNK
             return (
                 picked[z, c // 2][:, lo : lo + CHUNK].bitcast(FP8X4),
-                x_plane[:, z * S + c * CHUNK : z * S + (c + 1) * CHUNK],
+                x_plane[8 * z : P, c * CHUNK : (c + 1) * CHUNK],
             )
 
         w2_codes, w2_plane = {}, {}
 
         def quantize_w2(z):
-            grouped = []
             src = w2_raw[z][:].rearrange("p j (m t) -> p m j t", t=PACK)
-            for u in range(2):
-                g = tile("w2_bf%d_%d" % (z, u), [P, 2 * P * PACK], BF16)
-                dst = g[:].rearrange("p (t m j) -> p m j t", t=2, j=PACK)
-                if u == 0:
-                    nc.vector.tensor_copy(dst, src[:, :, :, 0:2])
-                else:
-                    nc.scalar.copy(dst, src[:, :, :, 2:4])
-                grouped.append(g)
+            grouped = tile("w2_bf%d" % z, [P, H * PACK], BF16)
+            dst = grouped[:].rearrange("p (t m j) -> p m j t", t=PACK, j=PACK)
+            nc.scalar.copy(dst[:, 0:SCALAR_M], src[:, 0:SCALAR_M])
+            nc.vector.tensor_copy(dst[:, SCALAR_M:P], src[:, SCALAR_M:P])
             for u in range(2):
                 w2_codes[z, u] = tile("w2_codes%d_%d" % (z, u), [P, 2 * P], U32)
                 w2_plane[z, u] = tile("w2_plane%d_%d" % (z, u), [P, 2 * P], U8)
-                nc.vector.quantize_mx(out=w2_codes[z, u][:].bitcast(FP8X4), scales=w2_plane[z, u][:], in_=grouped[u][:])
+                nc.vector.quantize_mx(
+                    out=w2_codes[z, u][:].bitcast(FP8X4),
+                    scales=w2_plane[z, u][:],
+                    in_=grouped[:, u * 1024 : (u + 1) * 1024],
+                )
 
         h_acc = [ps.tile([P, PACK, CHUNK], F32, name="h_acc%d" % c, tag="h_acc%d" % c) for c in range(CHUNKS)]
         o_acc = [ps.tile([P, M_TILES, CHUNK], F32, name="o_acc%d" % c, tag="o_acc%d" % c) for c in range(CHUNKS)]
@@ -135,6 +130,11 @@ def tile_picked_phlora_gelu_p_kernel(
 
         gather_words(0)
         quantize_w2(0)
+        w13 = tile("w13", [P, PASSES + 1, N], U32, tag="first_w2")
+        nc.sync.dma_start(
+            w13[:].bitcast(I32)[:, 0:PASSES, :], w1_words.rearrange("z p n t -> p z (n t)").bitcast(I32)
+        )
+        nc.sync.dma_start(w13[:].bitcast(I32)[:, PASSES, :], w3_words[0].rearrange("p n t -> p (n t)").bitcast(I32))
         for c in range(CHUNKS):
             hidden_pass(0, c)
         quantize_w2(1)
@@ -161,7 +161,7 @@ def tile_picked_phlora_gelu_p_kernel(
                     nc.tensor.matmul_mx(
                         out=o_acc[c][:, m, :],
                         lhsT=w13[:, z, cols].bitcast(FP8X4),
-                        lhsT_scale=w1_plane[4 * z : P, cols],
+                        lhsT_scale=w1_plane[:, z, cols],
                         rhs=rhs,
                         rhs_scale=rhs_scale,
                         start=(z == 0 and m == 0),

@@ -21,7 +21,7 @@ CHUNK = 128
 CHUNKS = S // CHUNK
 HALF = 256
 M_TILES = N // P
-SCALAR_M = 48
+SCALAR_M = (32, 32)
 
 
 def tile_picked_phlora_gelu_p_kernel(
@@ -40,34 +40,25 @@ def tile_picked_phlora_gelu_p_kernel(
         byte_win = tile("byte_win", [P, T], U8)
         nc.gpsimd.memset(byte_win[:].bitcast(I32), 0)
 
-        word_win = [tile("word_win0", [P, T], U32, tag="words")]
+        word_win = [tile("word_win0", [P, T], U32)]
         x_words32 = x_words.rearrange("z p n t -> z p (n t)").bitcast(I32)
         nc.sync.dma_start(word_win[0][:].bitcast(I32)[:, 0:512], x_words32[0, :, 0:512])
         nc.sync.dma_start(offsets[:], offs)
-        nc.sync.dma_start(word_win[0][:].bitcast(I32)[:, 512:1024], x_words32[0, :, 512:1024])
+        nc.sync.dma_start(word_win[0][:].bitcast(I32)[:, 512:1536], x_words32[0, :, 512:1536])
         x_rows = x_scales.bitcast(I32).rearrange("z (r e) c -> e r z c", e=2)
         for e in range(2):
             nc.sync.dma_start(byte_win[:].bitcast(I32)[e:P:8, :], x_rows[e])
-        nc.sync.dma_start(word_win[0][:].bitcast(I32)[:, 1024:T], x_words32[0, :, 1024:T])
+        nc.sync.dma_start(word_win[0][:].bitcast(I32)[:, 1536:T], x_words32[0, :, 1536:T])
+        w2_rows = w2.rearrange("(z p j) c -> z p j c", p=P, j=PACK)
+        w2_raw = [tile("w2_raw%d" % z, [P, PACK, H], F32) for z in range(PASSES)]
+        for z in range(PASSES):
+            nc.sync.dma_start(w2_raw[z][:], w2_rows[z])
 
-        def load_w2(z, tag):
-            raw = tile("w2_raw%d" % z, [P, PACK, H], F32, tag=tag)
-            nc.sync.dma_start(raw[:], w2[z * 512 : (z + 1) * 512, :].rearrange("(p j) c -> p j c", j=PACK))
-            return raw
-
-        w2_raw = [load_w2(0, "first_w2"), load_w2(1, "second_w2")]
-
-        w1_plane = tile("w1_plane", [P, PASSES, N], U8)
-        w3_plane = tile("w3_plane", [P, N], U8)
+        w1_plane = tile("w1_plane", [P, PASSES * N], U8)
         nc.gpsimd.memset(w1_plane[:].bitcast(I32), 0)
-        nc.gpsimd.memset(w3_plane[:].bitcast(I32), 0)
         w1_rows = w1_scales.bitcast(I32).rearrange("z q c -> q z c")
         for q in range(4):
-            nc.gpsimd.dma_start(w1_plane[:].bitcast(I32)[32 * q : 32 * q + 4, :, :], w1_rows[4 * q : 4 * q + 4])
-        for q in range(4):
-            nc.gpsimd.dma_start(
-                w3_plane[:].bitcast(I32)[32 * q : 32 * q + 4, :], w3_scales.bitcast(I32)[0, 4 * q : 4 * q + 4, :]
-            )
+            nc.gpsimd.dma_start(w1_plane[:].bitcast(I32)[32 * q : 32 * q + 4, :], w1_rows[4 * q : 4 * q + 4])
 
         picked_bytes = tile("picked_bytes", [P, S], U8, tag="last_words")
         nc.vector.tensor_copy(picked_bytes[:], byte_win[:].indirect(offsets[:]))
@@ -87,11 +78,11 @@ def tile_picked_phlora_gelu_p_kernel(
                 picked[z, u] = tile("picked%d_%d" % (z, u), [P, HALF], U32)
                 nc.vector.tensor_copy(picked[z, u][:], word_win[z][:].indirect(offsets[:, u * 16 : (u + 1) * 16]))
 
-        def tokens(z, c):
-            lo = (c % 2) * CHUNK
+        def tokens(z, first, width):
+            lo = first % HALF
             return (
-                picked[z, c // 2][:, lo : lo + CHUNK].bitcast(FP8X4),
-                x_plane[8 * z : P, c * CHUNK : (c + 1) * CHUNK],
+                picked[z, first // HALF][:, lo : lo + width].bitcast(FP8X4),
+                x_plane[8 * z : P, first : first + width],
             )
 
         w2_codes, w2_plane = {}, {}
@@ -100,8 +91,10 @@ def tile_picked_phlora_gelu_p_kernel(
             src = w2_raw[z][:].rearrange("p j (m t) -> p m j t", t=PACK)
             grouped = tile("w2_bf%d" % z, [P, H * PACK], BF16)
             dst = grouped[:].rearrange("p (t m j) -> p m j t", t=PACK, j=PACK)
-            nc.scalar.copy(dst[:, 0:SCALAR_M], src[:, 0:SCALAR_M])
-            nc.vector.tensor_copy(dst[:, SCALAR_M:P], src[:, SCALAR_M:P])
+            split = SCALAR_M[z]
+            if split:
+                nc.scalar.copy(dst[:, 0:split], src[:, 0:split])
+            nc.vector.tensor_copy(dst[:, split:P], src[:, split:P])
             for u in range(2):
                 w2_codes[z, u] = tile("w2_codes%d_%d" % (z, u), [P, 2 * P], U32)
                 w2_plane[z, u] = tile("w2_plane%d_%d" % (z, u), [P, 2 * P], U8)
@@ -112,10 +105,9 @@ def tile_picked_phlora_gelu_p_kernel(
                 )
 
         h_acc = [ps.tile([P, PACK, CHUNK], F32, name="h_acc%d" % c, tag="h_acc%d" % c) for c in range(CHUNKS)]
-        o_acc = [ps.tile([P, M_TILES, CHUNK], F32, name="o_acc%d" % c, tag="o_acc%d" % c) for c in range(CHUNKS)]
 
         def hidden_pass(z, c):
-            rhs, rhs_scale = tokens(z, c)
+            rhs, rhs_scale = tokens(z, c * CHUNK, CHUNK)
             for t in range(PACK):
                 cols = slice((t % 2) * P, (t % 2 + 1) * P)
                 nc.tensor.matmul_mx(
@@ -130,11 +122,17 @@ def tile_picked_phlora_gelu_p_kernel(
 
         gather_words(0)
         quantize_w2(0)
-        w13 = tile("w13", [P, PASSES + 1, N], U32, tag="first_w2")
+        w13 = tile("w13", [P, PASSES + 1, N], U32, tag="w2_raw0")
         nc.sync.dma_start(
             w13[:].bitcast(I32)[:, 0:PASSES, :], w1_words.rearrange("z p n t -> p z (n t)").bitcast(I32)
         )
         nc.sync.dma_start(w13[:].bitcast(I32)[:, PASSES, :], w3_words[0].rearrange("p n t -> p (n t)").bitcast(I32))
+        w3_plane = tile("w3_plane", [P, N], U8, tag="w2_bf0")
+        nc.vector.memset(w3_plane[:].bitcast(I32), 0)
+        for q in range(4):
+            nc.sync.dma_start(
+                w3_plane[:].bitcast(I32)[32 * q : 32 * q + 4, :], w3_scales.bitcast(I32)[0, 4 * q : 4 * q + 4, :]
+            )
         for c in range(CHUNKS):
             hidden_pass(0, c)
         quantize_w2(1)
@@ -144,7 +142,8 @@ def tile_picked_phlora_gelu_p_kernel(
 
         out_view = out.rearrange("(m p) n -> p m n", p=P)
         h_codes, h_plane = [], []
-        for c in range(CHUNKS):
+
+        def hidden_values(c):
             h_bf = tile("h_bf%d" % c, [P, CHUNK * PACK], BF16)
             nc.scalar.activation(
                 h_bf[:].rearrange("p (n t) -> p n t", t=PACK), h_acc[c][:].rearrange("p t n -> p n t"), GELU
@@ -153,31 +152,44 @@ def tile_picked_phlora_gelu_p_kernel(
             h_plane.append(tile("h_plane%d" % c, [P, CHUNK], U8))
             nc.vector.quantize_mx(out=h_codes[c][:].bitcast(FP8X4), scales=h_plane[c][:], in_=h_bf[:])
 
-        for c in range(CHUNKS):
+        def finish(chunks, row_tiles, bank, copy, queue):
+            first, width = chunks[0] * CHUNK, len(chunks) * CHUNK
+            name = "%d_%d" % (chunks[0], row_tiles[0])
+            acc = ps.tile([P, len(row_tiles), width], F32, name="o_acc" + name, tag=bank)
             for z in range(PASSES):
-                rhs, rhs_scale = tokens(z, c)
-                for m in range(M_TILES):
-                    cols = slice(m * P, (m + 1) * P)
+                rhs, rhs_scale = tokens(z, first, width)
+                for i, m in enumerate(row_tiles):
                     nc.tensor.matmul_mx(
-                        out=o_acc[c][:, m, :],
-                        lhsT=w13[:, z, cols].bitcast(FP8X4),
-                        lhsT_scale=w1_plane[:, z, cols],
+                        out=acc[:, i, :],
+                        lhsT=w13[:, z, m * P : (m + 1) * P].bitcast(FP8X4),
+                        lhsT_scale=w1_plane[:, z * N + m * P : z * N + (m + 1) * P],
                         rhs=rhs,
                         rhs_scale=rhs_scale,
-                        start=(z == 0 and m == 0),
+                        start=(z == 0 and i == 0),
                         stop=False,
                     )
-            for m in range(M_TILES):
-                cols = slice(m * P, (m + 1) * P)
-                nc.tensor.matmul_mx(
-                    out=o_acc[c][:, m, :],
-                    lhsT=w13[:, PASSES, cols].bitcast(FP8X4),
-                    lhsT_scale=w3_plane[:, cols],
-                    rhs=h_codes[c][:].bitcast(FP8X4),
-                    rhs_scale=h_plane[c][:],
-                    start=False,
-                    stop=(m == M_TILES - 1),
-                )
-            result = tile("result%d" % c, [P, M_TILES, CHUNK], F32)
-            nc.vector.tensor_copy(result[:], o_acc[c][:])
-            nc.sync.dma_start(out_view[:, :, c * CHUNK : (c + 1) * CHUNK], result[:])
+            for c in chunks:
+                for i, m in enumerate(row_tiles):
+                    nc.tensor.matmul_mx(
+                        out=acc[:, i, c * CHUNK - first : (c + 1) * CHUNK - first],
+                        lhsT=w13[:, PASSES, m * P : (m + 1) * P].bitcast(FP8X4),
+                        lhsT_scale=w3_plane[:, m * P : (m + 1) * P],
+                        rhs=h_codes[c][:].bitcast(FP8X4),
+                        rhs_scale=h_plane[c][:],
+                        start=False,
+                        stop=(c == chunks[-1] and m == row_tiles[-1]),
+                    )
+            result = tile("result" + name, [P, len(row_tiles), width], F32)
+            copy(result[:], acc[:])
+            rows = slice(row_tiles[0], row_tiles[-1] + 1)
+            queue.dma_start(out_view[:, rows, first : first + width], result[:])
+
+        hidden_values(0)
+        hidden_values(1)
+        hidden_values(2)
+        finish((0, 1), (0,), "h_acc0", nc.vector.tensor_copy, nc.sync)
+        finish((0, 1), (1,), "o_acc0", nc.vector.tensor_copy, nc.sync)
+        hidden_values(3)
+        finish((2,), (0, 1), "h_acc1", nc.scalar.copy, nc.sync)
+        finish((3,), (0,), "h_acc2", nc.vector.tensor_copy, nc.sync)
+        finish((3,), (1,), "o_acc1", nc.scalar.copy, nc.scalar)

@@ -21,7 +21,7 @@ CHUNK = 128
 CHUNKS = S // CHUNK
 HALF = 256
 M_TILES = N // P
-SCALAR_M = (32, 32)
+SCALAR_M = (40, 48)
 
 
 def tile_picked_phlora_gelu_p_kernel(
@@ -30,6 +30,7 @@ def tile_picked_phlora_gelu_p_kernel(
     nc = tc.nc
     with ExitStack() as ctx:
         sb = ctx.enter_context(tc.tile_pool(name="sb", bufs=1))
+        late = ctx.enter_context(tc.tile_pool(name="late", bufs=1))
         ps = ctx.enter_context(tc.psum_pool(name="ps", bufs=1))
 
         def tile(name, shape, dtype, tag=None):
@@ -37,18 +38,21 @@ def tile_picked_phlora_gelu_p_kernel(
 
         offsets = tile("offsets", [P, S // 16], U16)
 
+        warm = tile("warm", [P, 2], F32)
+        nc.vector.memset(warm[:, 0:1], 0.0)
+        nc.scalar.activation(warm[:, 1:2], warm[:, 0:1], GELU)
+
         byte_win = tile("byte_win", [P, T], U8)
-        nc.gpsimd.memset(byte_win[:].bitcast(I32), 0)
+        nc.vector.memset(byte_win[:].bitcast(I32), 0)
 
         word_win = [tile("word_win0", [P, T], U32)]
         x_words32 = x_words.rearrange("z p n t -> z p (n t)").bitcast(I32)
-        nc.sync.dma_start(word_win[0][:].bitcast(I32)[:, 0:512], x_words32[0, :, 0:512])
+        nc.sync.dma_start(word_win[0][:].bitcast(I32)[:, 0 : T // 2], x_words32[0, :, 0 : T // 2])
         nc.sync.dma_start(offsets[:], offs)
-        nc.sync.dma_start(word_win[0][:].bitcast(I32)[:, 512:1536], x_words32[0, :, 512:1536])
         x_rows = x_scales.bitcast(I32).rearrange("z (r e) c -> e r z c", e=2)
         for e in range(2):
             nc.sync.dma_start(byte_win[:].bitcast(I32)[e:P:8, :], x_rows[e])
-        nc.sync.dma_start(word_win[0][:].bitcast(I32)[:, 1536:T], x_words32[0, :, 1536:T])
+        nc.sync.dma_start(word_win[0][:].bitcast(I32)[:, T // 2 : T], x_words32[0, :, T // 2 : T])
         w2_rows = w2.rearrange("(z p j) c -> z p j c", p=P, j=PACK)
         w2_raw = [tile("w2_raw%d" % z, [P, PACK, H], F32) for z in range(PASSES)]
         for z in range(PASSES):
@@ -60,7 +64,7 @@ def tile_picked_phlora_gelu_p_kernel(
         for q in range(4):
             nc.gpsimd.dma_start(w1_plane[:].bitcast(I32)[32 * q : 32 * q + 4, :], w1_rows[4 * q : 4 * q + 4])
 
-        picked_bytes = tile("picked_bytes", [P, S], U8, tag="last_words")
+        picked_bytes = late.tile([P, S], U8, name="picked_bytes", align_bytes=64, offset=4 * T - S // 2)
         nc.vector.tensor_copy(picked_bytes[:], byte_win[:].indirect(offsets[:]))
         x_plane = tile("x_plane", [P, S], U8)
         x_plane32 = x_plane[:].bitcast(I32)
@@ -68,8 +72,13 @@ def tile_picked_phlora_gelu_p_kernel(
         for z in range(PASSES):
             for e in range(2):
                 nc.sync.dma_start(x_plane32[8 * z + 2 + e : P : 32, :], x_plane32[8 * z + 16 + e : P : 32, :])
-        word_win.append(tile("word_win1", [P, T], U32, tag="last_words"))
+        word_win.append(late.tile([P, T], U32, name="word_win1", align_bytes=64, offset=0))
         nc.sync.dma_start(word_win[1][:].bitcast(I32), x_words32[1])
+        w13 = late.tile([P, PASSES + 1, N], U32, name="w13", align_bytes=64, offset=4 * T)
+        nc.sync.dma_start(
+            w13[:].bitcast(I32)[:, 0:PASSES, :], w1_words.rearrange("z p n t -> p z (n t)").bitcast(I32)
+        )
+        nc.sync.dma_start(w13[:].bitcast(I32)[:, PASSES, :], w3_words[0].rearrange("p n t -> p (n t)").bitcast(I32))
 
         picked = {}
 
@@ -122,16 +131,22 @@ def tile_picked_phlora_gelu_p_kernel(
 
         gather_words(0)
         quantize_w2(0)
-        w13 = tile("w13", [P, PASSES + 1, N], U32, tag="w2_raw0")
-        nc.sync.dma_start(
-            w13[:].bitcast(I32)[:, 0:PASSES, :], w1_words.rearrange("z p n t -> p z (n t)").bitcast(I32)
-        )
-        nc.sync.dma_start(w13[:].bitcast(I32)[:, PASSES, :], w3_words[0].rearrange("p n t -> p (n t)").bitcast(I32))
-        w3_plane = tile("w3_plane", [P, N], U8, tag="w2_bf0")
+        w3_plane = tile("w3_plane", [P, N], U8, tag="w2_raw0")
         nc.vector.memset(w3_plane[:].bitcast(I32), 0)
         for q in range(4):
             nc.sync.dma_start(
                 w3_plane[:].bitcast(I32)[32 * q : 32 * q + 4, :], w3_scales.bitcast(I32)[0, 4 * q : 4 * q + 4, :]
+            )
+        idle = ps.tile([P, HALF], F32, name="idle", tag="o_acc3")
+        for warm_pass in range(4):
+            nc.tensor.matmul_mx(
+                out=idle[:],
+                lhsT=w2_codes[0, 0][:, 0:P].bitcast(FP8X4),
+                lhsT_scale=w2_plane[0, 0][:, 0:P],
+                rhs=w2_codes[0, 0][:].bitcast(FP8X4),
+                rhs_scale=w2_plane[0, 0][:],
+                start=True,
+                stop=True,
             )
         for c in range(CHUNKS):
             hidden_pass(0, c)
@@ -141,55 +156,60 @@ def tile_picked_phlora_gelu_p_kernel(
             hidden_pass(1, c)
 
         out_view = out.rearrange("(m p) n -> p m n", p=P)
-        h_codes, h_plane = [], []
+        h_codes, h_plane, results = [], [], []
 
         def hidden_values(c):
             h_bf = tile("h_bf%d" % c, [P, CHUNK * PACK], BF16)
             nc.scalar.activation(
                 h_bf[:].rearrange("p (n t) -> p n t", t=PACK), h_acc[c][:].rearrange("p t n -> p n t"), GELU
             )
-            h_codes.append(tile("h_codes%d" % c, [P, CHUNK], U32))
+            h_codes.append(tile("h_codes%d" % c, [P, CHUNK], U32, tag="h_codes%d" % (1 if c == 3 else c)))
             h_plane.append(tile("h_plane%d" % c, [P, CHUNK], U8))
             nc.vector.quantize_mx(out=h_codes[c][:].bitcast(FP8X4), scales=h_plane[c][:], in_=h_bf[:])
 
-        def finish(chunks, row_tiles, bank, copy, queue):
-            first, width = chunks[0] * CHUNK, len(chunks) * CHUNK
-            name = "%d_%d" % (chunks[0], row_tiles[0])
-            acc = ps.tile([P, len(row_tiles), width], F32, name="o_acc" + name, tag=bank)
-            for z in range(PASSES):
-                rhs, rhs_scale = tokens(z, first, width)
-                for i, m in enumerate(row_tiles):
-                    nc.tensor.matmul_mx(
-                        out=acc[:, i, :],
-                        lhsT=w13[:, z, m * P : (m + 1) * P].bitcast(FP8X4),
-                        lhsT_scale=w1_plane[:, z * N + m * P : z * N + (m + 1) * P],
-                        rhs=rhs,
-                        rhs_scale=rhs_scale,
-                        start=(z == 0 and i == 0),
-                        stop=False,
-                    )
-            for c in chunks:
-                for i, m in enumerate(row_tiles):
-                    nc.tensor.matmul_mx(
-                        out=acc[:, i, c * CHUNK - first : (c + 1) * CHUNK - first],
-                        lhsT=w13[:, PASSES, m * P : (m + 1) * P].bitcast(FP8X4),
-                        lhsT_scale=w3_plane[:, m * P : (m + 1) * P],
-                        rhs=h_codes[c][:].bitcast(FP8X4),
-                        rhs_scale=h_plane[c][:],
-                        start=False,
-                        stop=(c == chunks[-1] and m == row_tiles[-1]),
-                    )
-            result = tile("result" + name, [P, len(row_tiles), width], F32)
+        def finish(c, row_tiles, bank, copy, queue):
+            first = c * CHUNK
+            name = "%d_%d" % (c, row_tiles[0])
+            acc = ps.tile([P, len(row_tiles), CHUNK], F32, name="o_acc" + name, tag=bank)
+            direct = [
+                (i, w13[:, z, m * P : (m + 1) * P], w1_plane[:, z * N + m * P : z * N + (m + 1) * P])
+                + tokens(z, first, CHUNK)
+                for z in range(PASSES)
+                for i, m in enumerate(row_tiles)
+            ]
+            adapter = [
+                (
+                    i,
+                    w13[:, PASSES, m * P : (m + 1) * P],
+                    w3_plane[:, m * P : (m + 1) * P],
+                    h_codes[c][:].bitcast(FP8X4),
+                    h_plane[c][:],
+                )
+                for i, m in enumerate(row_tiles)
+            ]
+            passes = direct + adapter if c == CHUNKS - 1 else adapter + direct
+            for n, (i, words, plane, rhs, rhs_scale) in enumerate(passes):
+                nc.tensor.matmul_mx(
+                    out=acc[:, i, :],
+                    lhsT=words.bitcast(FP8X4),
+                    lhsT_scale=plane,
+                    rhs=rhs,
+                    rhs_scale=rhs_scale,
+                    start=(n == 0),
+                    stop=(n == len(passes) - 1),
+                )
+            result = tile("result" + name, [P, len(row_tiles), CHUNK], F32)
             copy(result[:], acc[:])
+            results.append(result)
             rows = slice(row_tiles[0], row_tiles[-1] + 1)
-            queue.dma_start(out_view[:, rows, first : first + width], result[:])
+            queue.dma_start(out_view[:, rows, first : first + CHUNK], result[:])
 
-        hidden_values(0)
-        hidden_values(1)
+        for c in range(2):
+            hidden_values(c)
+        finish(0, (0, 1), "o_acc0", nc.vector.tensor_copy, nc.sync)
         hidden_values(2)
-        finish((0, 1), (0,), "h_acc0", nc.vector.tensor_copy, nc.sync)
-        finish((0, 1), (1,), "o_acc0", nc.vector.tensor_copy, nc.sync)
+        finish(1, (0, 1), "o_acc1", nc.scalar.copy, nc.sync)
         hidden_values(3)
-        finish((2,), (0, 1), "h_acc1", nc.scalar.copy, nc.sync)
-        finish((3,), (0,), "h_acc2", nc.vector.tensor_copy, nc.sync)
-        finish((3,), (1,), "o_acc1", nc.scalar.copy, nc.scalar)
+        finish(2, (0, 1), "o_acc2", nc.scalar.copy, nc.sync)
+        finish(3, (0,), "o_acc3", nc.vector.tensor_copy, nc.sync)
+        finish(3, (1,), "h_acc0", nc.scalar.copy, nc.scalar)

@@ -163,7 +163,7 @@ def tile_picked_phlora_gelu_p_kernel(
             nc.scalar.activation(
                 h_bf[:].rearrange("p (n t) -> p n t", t=PACK), h_acc[c][:].rearrange("p t n -> p n t"), GELU
             )
-            h_codes.append(tile("h_codes%d" % c, [P, CHUNK], U32, tag="h_codes%d" % (1 if c == 3 else c)))
+            h_codes.append(tile("h_codes%d" % c, [P, CHUNK], U32))
             h_plane.append(tile("h_plane%d" % c, [P, CHUNK], U8))
             nc.vector.quantize_mx(out=h_codes[c][:].bitcast(FP8X4), scales=h_plane[c][:], in_=h_bf[:])
 
@@ -187,7 +187,7 @@ def tile_picked_phlora_gelu_p_kernel(
                 )
                 for i, m in enumerate(row_tiles)
             ]
-            passes = direct + adapter if c == CHUNKS - 1 else adapter + direct
+            passes = adapter + direct if c == 1 else direct + adapter
             for n, (i, words, plane, rhs, rhs_scale) in enumerate(passes):
                 nc.tensor.matmul_mx(
                     out=acc[:, i, :],
@@ -204,12 +204,10 @@ def tile_picked_phlora_gelu_p_kernel(
             rows = slice(row_tiles[0], row_tiles[-1] + 1)
             queue.dma_start(out_view[:, rows, first : first + CHUNK], result[:])
 
-        for c in range(2):
+        for c in range(CHUNKS):
             hidden_values(c)
-        finish(0, (0, 1), "o_acc0", nc.vector.tensor_copy, nc.sync)
-        hidden_values(2)
+        finish(0, (0, 1), "o_acc0", nc.scalar.copy, nc.sync)
         finish(1, (0, 1), "o_acc1", nc.scalar.copy, nc.sync)
-        hidden_values(3)
-        finish(2, (0, 1), "o_acc2", nc.scalar.copy, nc.sync)
+        finish(2, (0, 1), "o_acc2", nc.vector.tensor_copy, nc.sync)
         finish(3, (0,), "o_acc3", nc.vector.tensor_copy, nc.sync)
         finish(3, (1,), "h_acc0", nc.scalar.copy, nc.scalar)

@@ -58,27 +58,26 @@ def tile_picked_phlora_gelu_p_kernel(
         for z in range(PASSES):
             nc.sync.dma_start(w2_raw[z][:], w2_rows[z])
 
-        w1_plane = tile("w1_plane", [P, PASSES * N], U8)
-        nc.gpsimd.memset(w1_plane[:].bitcast(I32), 0)
-        w1_rows = w1_scales.bitcast(I32).rearrange("z q c -> q z c")
-        for q in range(4):
-            nc.gpsimd.dma_start(w1_plane[:].bitcast(I32)[32 * q : 32 * q + 4, :], w1_rows[4 * q : 4 * q + 4])
-
         picked_bytes = late.tile([P, S], U8, name="picked_bytes", align_bytes=64, offset=4 * T - S // 2)
         nc.vector.tensor_copy(picked_bytes[:], byte_win[:].indirect(offsets[:]))
-        x_plane = tile("x_plane", [P, S], U8)
-        x_plane32 = x_plane[:].bitcast(I32)
-        nc.vector.tensor_copy(x_plane32, picked_bytes[:].bitcast(I32))
+        x_plane = [tile("x_plane%d" % z, [P, S], U8) for z in range(PASSES)]
         for z in range(PASSES):
+            nc.vector.tensor_copy(x_plane[z][:].bitcast(I32), picked_bytes[:].bitcast(I32))
+
+        def move_odd_rows(z):
+            rows = x_plane[z][:].bitcast(I32)
             for e in range(2):
-                nc.sync.dma_start(x_plane32[8 * z + 2 + e : P : 32, :], x_plane32[8 * z + 16 + e : P : 32, :])
+                nc.sync.dma_start(rows[8 * z + 2 + e : P : 32, :], rows[8 * z + 16 + e : P : 32, :])
+
+        move_odd_rows(0)
         word_win.append(late.tile([P, T], U32, name="word_win1", align_bytes=64, offset=0))
         nc.sync.dma_start(word_win[1][:].bitcast(I32), x_words32[1])
-        w13 = late.tile([P, PASSES + 1, N], U32, name="w13", align_bytes=64, offset=4 * T)
-        nc.sync.dma_start(
-            w13[:].bitcast(I32)[:, 0:PASSES, :], w1_words.rearrange("z p n t -> p z (n t)").bitcast(I32)
-        )
-        nc.sync.dma_start(w13[:].bitcast(I32)[:, PASSES, :], w3_words[0].rearrange("p n t -> p (n t)").bitcast(I32))
+        move_odd_rows(1)
+        w1_plane = late.tile([P, PASSES * N], U8, name="w1_plane", align_bytes=64, offset=4 * T)
+        nc.vector.memset(w1_plane[:].bitcast(I32), 0)
+        w1_rows = w1_scales.bitcast(I32).rearrange("z q c -> q z c")
+        for q in range(4):
+            nc.sync.dma_start(w1_plane[:].bitcast(I32)[32 * q : 32 * q + 4, :], w1_rows[4 * q : 4 * q + 4])
 
         picked = {}
 
@@ -91,7 +90,7 @@ def tile_picked_phlora_gelu_p_kernel(
             lo = first % HALF
             return (
                 picked[z, first // HALF][:, lo : lo + width].bitcast(FP8X4),
-                x_plane[8 * z : P, first : first + width],
+                x_plane[z][8 * z : P, first : first + width],
             )
 
         w2_codes, w2_plane = {}, {}
@@ -131,7 +130,12 @@ def tile_picked_phlora_gelu_p_kernel(
 
         gather_words(0)
         quantize_w2(0)
-        w3_plane = tile("w3_plane", [P, N], U8, tag="w2_raw0")
+        w13 = tile("w13", [P, PASSES + 1, N], U32, tag="w2_raw0")
+        nc.sync.dma_start(
+            w13[:].bitcast(I32)[:, 0:PASSES, :], w1_words.rearrange("z p n t -> p z (n t)").bitcast(I32)
+        )
+        nc.sync.dma_start(w13[:].bitcast(I32)[:, PASSES, :], w3_words[0].rearrange("p n t -> p (n t)").bitcast(I32))
+        w3_plane = tile("w3_plane", [P, N], U8, tag="w2_bf0")
         nc.vector.memset(w3_plane[:].bitcast(I32), 0)
         for q in range(4):
             nc.sync.dma_start(

@@ -141,17 +141,6 @@ def tile_picked_phlora_gelu_p_kernel(
             nc.sync.dma_start(
                 w3_plane[:].bitcast(I32)[32 * q : 32 * q + 4, :], w3_scales.bitcast(I32)[0, 4 * q : 4 * q + 4, :]
             )
-        idle = ps.tile([P, HALF], F32, name="idle", tag="o_acc3")
-        for warm_pass in range(4):
-            nc.tensor.matmul_mx(
-                out=idle[:],
-                lhsT=w2_codes[0, 0][:, 0:P].bitcast(FP8X4),
-                lhsT_scale=w2_plane[0, 0][:, 0:P],
-                rhs=w2_codes[0, 0][:].bitcast(FP8X4),
-                rhs_scale=w2_plane[0, 0][:],
-                start=True,
-                stop=True,
-            )
         for c in range(CHUNKS):
             hidden_pass(0, c)
         quantize_w2(1)

@@ -149,7 +149,7 @@ def tile_picked_phlora_gelu_p_kernel(
             hidden_pass(1, c)
 
         out_view = out.rearrange("(m p) n -> p m n", p=P)
-        h_codes, h_plane, results = [], [], []
+        h_codes, h_plane = [], []
 
         def hidden_values(c):
             h_bf = tile("h_bf%d" % c, [P, CHUNK * PACK], BF16)
@@ -160,30 +160,29 @@ def tile_picked_phlora_gelu_p_kernel(
             h_plane.append(tile("h_plane%d" % c, [P, CHUNK], U8))
             nc.vector.quantize_mx(out=h_codes[c][:].bitcast(FP8X4), scales=h_plane[c][:], in_=h_bf[:])
 
-        def finish(c, row_tiles, bank, copy, queue):
-            first = c * CHUNK
-            name = "%d_%d" % (c, row_tiles[0])
-            acc = ps.tile([P, len(row_tiles), CHUNK], F32, name="o_acc" + name, tag=bank)
-            direct = [
-                (i, w13[:, z, m * P : (m + 1) * P], w1_plane[:, z * N + m * P : z * N + (m + 1) * P])
-                + tokens(z, first, CHUNK)
+        def finish(chunks, row_tiles, bank, copy, queue):
+            first, width = chunks[0] * CHUNK, len(chunks) * CHUNK
+            name = "%d_%d" % (chunks[0], row_tiles[0])
+            acc = ps.tile([P, len(row_tiles), width], F32, name="o_acc" + name, tag=bank)
+            passes = [
+                (acc[:, i, :], w13[:, z, m * P : (m + 1) * P], w1_plane[:, z * N + m * P : z * N + (m + 1) * P])
+                + tokens(z, first, width)
                 for z in range(PASSES)
                 for i, m in enumerate(row_tiles)
-            ]
-            adapter = [
+            ] + [
                 (
-                    i,
+                    acc[:, i, c * CHUNK - first : (c + 1) * CHUNK - first],
                     w13[:, PASSES, m * P : (m + 1) * P],
                     w3_plane[:, m * P : (m + 1) * P],
                     h_codes[c][:].bitcast(FP8X4),
                     h_plane[c][:],
                 )
+                for c in chunks
                 for i, m in enumerate(row_tiles)
             ]
-            passes = adapter + direct if c == 1 else direct + adapter
-            for n, (i, words, plane, rhs, rhs_scale) in enumerate(passes):
+            for n, (sums, words, plane, rhs, rhs_scale) in enumerate(passes):
                 nc.tensor.matmul_mx(
-                    out=acc[:, i, :],
+                    out=sums,
                     lhsT=words.bitcast(FP8X4),
                     lhsT_scale=plane,
                     rhs=rhs,
@@ -191,16 +190,15 @@ def tile_picked_phlora_gelu_p_kernel(
                     start=(n == 0),
                     stop=(n == len(passes) - 1),
                 )
-            result = tile("result" + name, [P, len(row_tiles), CHUNK], F32)
+            result = tile("result" + name, [P, len(row_tiles), width], F32)
             copy(result[:], acc[:])
-            results.append(result)
             rows = slice(row_tiles[0], row_tiles[-1] + 1)
-            queue.dma_start(out_view[:, rows, first : first + CHUNK], result[:])
+            queue.dma_start(out_view[:, rows, first : first + width], result[:])
 
         for c in range(CHUNKS):
             hidden_values(c)
-        finish(0, (0, 1), "o_acc0", nc.scalar.copy, nc.sync)
-        finish(1, (0, 1), "o_acc1", nc.scalar.copy, nc.sync)
-        finish(2, (0, 1), "o_acc2", nc.vector.tensor_copy, nc.sync)
-        finish(3, (0,), "o_acc3", nc.vector.tensor_copy, nc.sync)
-        finish(3, (1,), "h_acc0", nc.scalar.copy, nc.scalar)
+        finish((0, 1), (0,), "o_acc0", nc.scalar.copy, nc.sync)
+        finish((0, 1), (1,), "o_acc1", nc.scalar.copy, nc.sync)
+        finish((2,), (0, 1), "o_acc2", nc.vector.tensor_copy, nc.sync)
+        finish((3,), (0,), "o_acc3", nc.vector.tensor_copy, nc.sync)
+        finish((3,), (1,), "h_acc0", nc.scalar.copy, nc.scalar)

@@ -22,6 +22,7 @@ CHUNKS = S // CHUNK
 HALF = 256
 M_TILES = N // P
 SCALAR_M = (40, 48)
+FIRST = 3 * T // 8
 
 
 def tile_picked_phlora_gelu_p_kernel(
@@ -38,21 +39,21 @@ def tile_picked_phlora_gelu_p_kernel(
 
         offsets = tile("offsets", [P, S // 16], U16)
 
+        byte_win = tile("byte_win", [P, T], U8)
+        nc.vector.memset(byte_win[:].bitcast(I32), 0)
+
         warm = tile("warm", [P, 2], F32)
         nc.vector.memset(warm[:, 0:1], 0.0)
         nc.scalar.activation(warm[:, 1:2], warm[:, 0:1], GELU)
 
-        byte_win = tile("byte_win", [P, T], U8)
-        nc.vector.memset(byte_win[:].bitcast(I32), 0)
-
         word_win = [tile("word_win0", [P, T], U32)]
         x_words32 = x_words.rearrange("z p n t -> z p (n t)").bitcast(I32)
-        nc.sync.dma_start(word_win[0][:].bitcast(I32)[:, 0 : T // 2], x_words32[0, :, 0 : T // 2])
+        nc.sync.dma_start(word_win[0][:].bitcast(I32)[:, 0:FIRST], x_words32[0, :, 0:FIRST])
         nc.sync.dma_start(offsets[:], offs)
         x_rows = x_scales.bitcast(I32).rearrange("z (r e) c -> e r z c", e=2)
         for e in range(2):
             nc.sync.dma_start(byte_win[:].bitcast(I32)[e:P:8, :], x_rows[e])
-        nc.sync.dma_start(word_win[0][:].bitcast(I32)[:, T // 2 : T], x_words32[0, :, T // 2 : T])
+        nc.sync.dma_start(word_win[0][:].bitcast(I32)[:, FIRST:T], x_words32[0, :, FIRST:T])
         w2_rows = w2.rearrange("(z p j) c -> z p j c", p=P, j=PACK)
         w2_raw = [tile("w2_raw%d" % z, [P, PACK, H], F32) for z in range(PASSES)]
         for z in range(PASSES):

@@ -161,7 +161,7 @@ def tile_picked_phlora_gelu_p_kernel(
             h_plane.append(tile("h_plane%d" % c, [P, CHUNK], U8))
             nc.vector.quantize_mx(out=h_codes[c][:].bitcast(FP8X4), scales=h_plane[c][:], in_=h_bf[:])
 
-        def finish(chunks, row_tiles, bank, copy, queue):
+        def finish(chunks, row_tiles, bank, copy):
             first, width = chunks[0] * CHUNK, len(chunks) * CHUNK
             name = "%d_%d" % (chunks[0], row_tiles[0])
             acc = ps.tile([P, len(row_tiles), width], F32, name="o_acc" + name, tag=bank)
@@ -191,15 +191,20 @@ def tile_picked_phlora_gelu_p_kernel(
                     start=(n == 0),
                     stop=(n == len(passes) - 1),
                 )
-            result = tile("result" + name, [P, len(row_tiles), width], F32)
-            copy(result[:], acc[:])
             rows = slice(row_tiles[0], row_tiles[-1] + 1)
-            queue.dma_start(out_view[:, rows, first : first + width], result[:])
+            lo = first % HALF
+            copy(result[first // HALF][:, rows, lo : lo + width], acc[:])
 
         for c in range(CHUNKS):
             hidden_values(c)
-        finish((0, 1), (0,), "o_acc0", nc.scalar.copy, nc.sync)
-        finish((0, 1), (1,), "o_acc1", nc.scalar.copy, nc.sync)
-        finish((2,), (0, 1), "o_acc2", nc.vector.tensor_copy, nc.sync)
-        finish((3,), (0,), "o_acc3", nc.vector.tensor_copy, nc.sync)
-        finish((3,), (1,), "h_acc0", nc.scalar.copy, nc.scalar)
+        result = [tile("result%d" % u, [P, M_TILES, HALF], F32) for u in range(S // HALF)]
+        finish((0, 1), (0,), "o_acc0", nc.scalar.copy)
+        for e in range(2):
+            nc.sync.dma_start(out_view[e:P:2, 0, 0:HALF], result[0][e:P:2, 0, :])
+        finish((0, 1), (1,), "o_acc1", nc.scalar.copy)
+        nc.sync.dma_start(out_view[:, 1, 0:HALF], result[0][:, 1, :])
+        finish((2,), (0, 1), "o_acc2", nc.vector.tensor_copy)
+        finish((3,), (0,), "o_acc3", nc.vector.tensor_copy)
+        nc.sync.dma_start(out_view[:, 0, HALF:S], result[1][:, 0, :])
+        finish((3,), (1,), "h_acc0", nc.scalar.copy)
+        nc.scalar.dma_start(out_view[:, 1, HALF:S], result[1][:, 1, :])

from contextlib import ExitStack

import concourse.mybir as mybir

K, T, S, H, N = 1024, 2048, 512, 512, 256
FLOPS = 2 * S * (K * H + K * N + H * N)

F32 = mybir.dt.float32
BF16 = mybir.dt.bfloat16
I32 = mybir.dt.int32
U32 = mybir.dt.uint32
U16 = mybir.dt.uint16
U8 = mybir.dt.uint8
FP8X4 = mybir.dt.float8_e4m3fn_x4
GELU = mybir.ActivationFunctionType.Gelu_apprx_tanh

P = 128
PACK = 4
PASSES = K // (P * PACK)
CHUNK = 128
CHUNKS = S // CHUNK
HALF = 256
M_TILES = N // P
SCALAR_M = (40, 48)
FIRST = 3 * T // 8


def tile_picked_phlora_gelu_p_kernel(
    tc, x_words, x_scales, w1_words, w1_scales, w2, w3_words, w3_scales, offs, out
):
    nc = tc.nc
    with ExitStack() as ctx:
        sb = ctx.enter_context(tc.tile_pool(name="sb", bufs=1))
        late = ctx.enter_context(tc.tile_pool(name="late", bufs=1))
        ps = ctx.enter_context(tc.psum_pool(name="ps", bufs=1))

        def tile(name, shape, dtype, tag=None):
            return sb.tile(shape, dtype, name=name, tag=tag or name, align_bytes=64)

        offsets = tile("offsets", [P, S // 16], U16)

        byte_win = tile("byte_win", [P, T], U8)
        nc.vector.memset(byte_win[:].bitcast(I32), 0)

        warm = tile("warm", [P, 2], F32)
        nc.vector.memset(warm[:, 0:1], 0.0)
        nc.scalar.activation(warm[:, 1:2], warm[:, 0:1], GELU)

        word_win = [tile("word_win0", [P, T], U32)]
        x_words32 = x_words.rearrange("z p n t -> z p (n t)").bitcast(I32)
        nc.sync.dma_start(word_win[0][:].bitcast(I32)[:, 0:FIRST], x_words32[0, :, 0:FIRST])
        nc.sync.dma_start(offsets[:], offs)
        x_rows = x_scales.bitcast(I32).rearrange("z (r e) c -> e r z c", e=2)
        for e in range(2):
            nc.sync.dma_start(byte_win[:].bitcast(I32)[e:P:8, :], x_rows[e])
        nc.sync.dma_start(word_win[0][:].bitcast(I32)[:, FIRST:T], x_words32[0, :, FIRST:T])
        w2_rows = w2.rearrange("(z p j) c -> z p j c", p=P, j=PACK)
        w2_raw = [tile("w2_raw%d" % z, [P, PACK, H], F32) for z in range(PASSES)]
        for z in range(PASSES):
            nc.sync.dma_start(w2_raw[z][:], w2_rows[z])

        picked_bytes = late.tile([P, S], U8, name="picked_bytes", align_bytes=64, offset=4 * T - S // 2)
        nc.vector.tensor_copy(picked_bytes[:], byte_win[:].indirect(offsets[:]))
        x_plane = [tile("x_plane%d" % z, [P, S], U8) for z in range(PASSES)]
        for z in range(PASSES):
            nc.vector.tensor_copy(x_plane[z][:].bitcast(I32), picked_bytes[:].bitcast(I32))

        def move_odd_rows(z):
            rows = x_plane[z][:].bitcast(I32)
            for e in range(2):
                nc.sync.dma_start(rows[8 * z + 2 + e : P : 32, :], rows[8 * z + 16 + e : P : 32, :])

        move_odd_rows(0)
        word_win.append(late.tile([P, T], U32, name="word_win1", align_bytes=64, offset=0))
        nc.sync.dma_start(word_win[1][:].bitcast(I32), x_words32[1])
        move_odd_rows(1)
        w1_plane = late.tile([P, PASSES * N], U8, name="w1_plane", align_bytes=64, offset=4 * T)
        nc.vector.memset(w1_plane[:].bitcast(I32), 0)
        w1_rows = w1_scales.bitcast(I32).rearrange("z q c -> q z c")
        for q in range(4):
            nc.sync.dma_start(w1_plane[:].bitcast(I32)[32 * q : 32 * q + 4, :], w1_rows[4 * q : 4 * q + 4])

        picked = {}

        def gather_words(z):
            for u in range(S // HALF):
                picked[z, u] = tile("picked%d_%d" % (z, u), [P, HALF], U32)
                nc.vector.tensor_copy(picked[z, u][:], word_win[z][:].indirect(offsets[:, u * 16 : (u + 1) * 16]))

        def tokens(z, first, width):
            lo = first % HALF
            return (
                picked[z, first // HALF][:, lo : lo + width].bitcast(FP8X4),
                x_plane[z][8 * z : P, first : first + width],
            )

        w2_codes, w2_plane = {}, {}

        def quantize_w2(z):
            src = w2_raw[z][:].rearrange("p j (m t) -> p m j t", t=PACK)
            grouped = tile("w2_bf%d" % z, [P, H * PACK], BF16)
            dst = grouped[:].rearrange("p (t m j) -> p m j t", t=PACK, j=PACK)
            split = SCALAR_M[z]
            if split:
                nc.scalar.copy(dst[:, 0:split], src[:, 0:split])
            nc.vector.tensor_copy(dst[:, split:P], src[:, split:P])
            for u in range(2):
                w2_codes[z, u] = tile("w2_codes%d_%d" % (z, u), [P, 2 * P], U32)
                w2_plane[z, u] = tile("w2_plane%d_%d" % (z, u), [P, 2 * P], U8)
                nc.vector.quantize_mx(
                    out=w2_codes[z, u][:].bitcast(FP8X4),
                    scales=w2_plane[z, u][:],
                    in_=grouped[:, u * 1024 : (u + 1) * 1024],
                )

        h_acc = [ps.tile([P, PACK, CHUNK], F32, name="h_acc%d" % c, tag="h_acc%d" % c) for c in range(CHUNKS)]

        def hidden_pass(z, c):
            rhs, rhs_scale = tokens(z, c * CHUNK, CHUNK)
            for t in range(PACK):
                cols = slice((t % 2) * P, (t % 2 + 1) * P)
                nc.tensor.matmul_mx(
                    out=h_acc[c][:, t, :],
                    lhsT=w2_codes[z, t // 2][:, cols].bitcast(FP8X4),
                    lhsT_scale=w2_plane[z, t // 2][:, cols],
                    rhs=rhs,
                    rhs_scale=rhs_scale,
                    start=(z == 0 and t == 0),
                    stop=(z == PASSES - 1 and t == PACK - 1),
                )

        gather_words(0)
        quantize_w2(0)
        w13 = tile("w13", [P, PASSES + 1, N], U32, tag="w2_raw0")
        nc.sync.dma_start(
            w13[:].bitcast(I32)[:, 0:PASSES, :], w1_words.rearrange("z p n t -> p z (n t)").bitcast(I32)
        )
        nc.sync.dma_start(w13[:].bitcast(I32)[:, PASSES, :], w3_words[0].rearrange("p n t -> p (n t)").bitcast(I32))
        w3_plane = tile("w3_plane", [P, N], U8, tag="w2_bf0")
        nc.vector.memset(w3_plane[:].bitcast(I32), 0)
        for q in range(4):
            nc.sync.dma_start(
                w3_plane[:].bitcast(I32)[32 * q : 32 * q + 4, :], w3_scales.bitcast(I32)[0, 4 * q : 4 * q + 4, :]
            )
        for c in range(CHUNKS):
            hidden_pass(0, c)
        quantize_w2(1)
        gather_words(1)
        for c in range(CHUNKS):
            hidden_pass(1, c)

        out_view = out.rearrange("(m p) n -> p m n", p=P)
        h_codes, h_plane = [], []

        def hidden_values(c):
            h_bf = tile("h_bf%d" % c, [P, CHUNK * PACK], BF16)
            nc.scalar.activation(
                h_bf[:].rearrange("p (n t) -> p n t", t=PACK), h_acc[c][:].rearrange("p t n -> p n t"), GELU
            )
            h_codes.append(tile("h_codes%d" % c, [P, CHUNK], U32))
            h_plane.append(tile("h_plane%d" % c, [P, CHUNK], U8))
            nc.vector.quantize_mx(out=h_codes[c][:].bitcast(FP8X4), scales=h_plane[c][:], in_=h_bf[:])

        def finish(chunks, row_tiles, bank, copy):
            first, width = chunks[0] * CHUNK, len(chunks) * CHUNK
            name = "%d_%d" % (chunks[0], row_tiles[0])
            acc = ps.tile([P, len(row_tiles), width], F32, name="o_acc" + name, tag=bank)
            passes = [
                (acc[:, i, :], w13[:, z, m * P : (m + 1) * P], w1_plane[:, z * N + m * P : z * N + (m + 1) * P])
                + tokens(z, first, width)
                for z in range(PASSES)
                for i, m in enumerate(row_tiles)
            ] + [
                (
                    acc[:, i, c * CHUNK - first : (c + 1) * CHUNK - first],
                    w13[:, PASSES, m * P : (m + 1) * P],
                    w3_plane[:, m * P : (m + 1) * P],
                    h_codes[c][:].bitcast(FP8X4),
                    h_plane[c][:],
                )
                for c in chunks
                for i, m in enumerate(row_tiles)
            ]
            for n, (sums, words, plane, rhs, rhs_scale) in enumerate(passes):
                nc.tensor.matmul_mx(
                    out=sums,
                    lhsT=words.bitcast(FP8X4),
                    lhsT_scale=plane,
                    rhs=rhs,
                    rhs_scale=rhs_scale,
                    start=(n == 0),
                    stop=(n == len(passes) - 1),
                )
            rows = slice(row_tiles[0], row_tiles[-1] + 1)
            lo = first % HALF
            copy(result[first // HALF][:, rows, lo : lo + width], acc[:])

        for c in range(CHUNKS):
            hidden_values(c)
        result = [tile("result%d" % u, [P, M_TILES, HALF], F32) for u in range(S // HALF)]
        finish((0, 1), (0,), "o_acc0", nc.scalar.copy)
        for e in range(2):
            nc.sync.dma_start(out_view[e:P:2, 0, 0:HALF], result[0][e:P:2, 0, :])
        finish((0, 1), (1,), "o_acc1", nc.scalar.copy)
        nc.sync.dma_start(out_view[:, 1, 0:HALF], result[0][:, 1, :])
        finish((2,), (0, 1), "o_acc2", nc.vector.tensor_copy)
        finish((3,), (0,), "o_acc3", nc.vector.tensor_copy)
        nc.sync.dma_start(out_view[:, 0, HALF:S], result[1][:, 0, :])
        finish((3,), (1,), "h_acc0", nc.scalar.copy)
        nc.scalar.dma_start(out_view[:, 1, HALF:S], result[1][:, 1, :])
